import numpy as np
import ml_dtypes


def mxq(x, axis, fmt="e4m3"):
    dtype, down = {"e4m3": (ml_dtypes.float8_e4m3fn, 7), "e5m2": (ml_dtypes.float8_e5m2, 14)}[fmt]
    v = np.moveaxis(np.asarray(x, np.float32).astype(ml_dtypes.bfloat16).astype(np.float64), axis, -1)
    blocks = v.reshape(v.shape[:-1] + (-1, 32))
    amax = np.abs(blocks).max(-1, keepdims=True)
    byte = np.maximum(np.where(amax > 0, np.frexp(amax)[1] - 1 + 127, 0) - down, 1)
    scale = np.exp2(byte - 127.0)
    codes = (blocks / scale).astype(np.float32).astype(dtype).astype(np.float64)
    return np.moveaxis((codes * scale).reshape(v.shape), -1, axis)


WIDE = False


def mx_kscale(k):
    if not WIDE:
        return np.ones(k)
    levels = np.array([10, -10, 5, -5, 0])
    if k % 512:
        return np.exp2(np.random.permutation(np.resize(levels, k // 32))).repeat(32)
    a = np.empty((k // 512, 16))
    for p in range(k // 512):
        a[p, :8] = np.random.permutation(np.resize(levels, 8))
        for g in range(8):
            far = levels[np.abs(levels - a[p, g]) >= 10]
            a[p, g + 8] = far[np.random.randint(len(far))]
    return np.exp2(a.ravel()).repeat(32)


def f64(x):
    return np.asarray(x).astype(np.float64)


def striped(idx):
    return np.tile(np.asarray(idx).reshape(-1, 16).T, (8, 1)).astype(np.uint16)


def unstriped(offs):
    return offs[:16].T.reshape(-1).astype(np.int64)


E2M1 = np.array([0.0, 0.5, 1.0, 1.5, 2.0, 3.0, 4.0, 6.0, -0.0, -0.5, -1.0, -1.5, -2.0, -3.0, -4.0, -6.0])


def pack_weight(w, fmt):
    k, n = w.shape
    w = f64(np.asarray(w, np.float32).astype(ml_dtypes.bfloat16)).reshape(k // 32, 32, n)
    amax = np.abs(w).max(1)
    if fmt == "e4m3":
        byte = np.frexp(amax)[1] - 1 + 127 - 7
    else:
        mant, ex = np.frexp(amax / 6.0)
        byte = np.where(mant > 0.5, ex, ex - 1) + 127
    byte = np.clip(np.where(amax > 0, byte, 1), 1, 254)
    scaled = (w * np.exp2(127.0 - byte)[:, None, :]).reshape(k, n).astype(np.float32)
    by_word = np.ascontiguousarray(scaled.reshape(k // 512, 128, 4, n).transpose(0, 1, 3, 2))
    if fmt == "e4m3":
        words = by_word.astype(ml_dtypes.float8_e4m3fn).view(np.uint8)
    else:
        c = by_word.astype(ml_dtypes.float4_e2m1fn).view(np.uint8) & 0xF
        words = (c[..., 0::2] | (c[..., 1::2] << 4)).reshape(k // 512, 128, 2 * n)
    return np.ascontiguousarray(words), np.ascontiguousarray(byte.astype(np.uint8).reshape(k // 512, 16, n))


def unpack_weight(words, scales, fmt):
    g, _, n = scales.shape
    words = np.ascontiguousarray(words).reshape(g, 128, n, -1)
    if fmt == "e4m3":
        vals = words.view(ml_dtypes.float8_e4m3fn).astype(np.float64)
    else:
        nib = np.empty((g, 128, n, 4), np.uint8)
        nib[..., 0::2] = words & 0xF
        nib[..., 1::2] = words >> 4
        vals = E2M1[nib]
    vals = vals * np.repeat(np.exp2(scales.astype(np.float64) - 127.0), 8, axis=1)[..., None]
    return vals.transpose(0, 1, 3, 2).reshape(g * 512, n)


K, R, F, T, J, M = 512, 128, 512, 2048, 512, 256


def setup_inputs():
    n = np.random.standard_normal
    idx = np.random.permutation(T)[:J]
    idx2 = np.random.permutation(J)[:M]
    idx3 = np.random.permutation(J)[:M]
    idx4 = np.random.permutation(J)[:M]
    fk = mx_kscale(K)
    dtabp = pack_weight(n((K, T)) / fk[:, None], "e4m3")
    tabp = pack_weight(n((K, T)) / fk[:, None], "e4m3")
    return {
        "dtab_words": dtabp[0],
        "dtab_scales": dtabp[1],
        "tab_words": tabp[0],
        "tab_scales": tabp[1],
        "w1": (n((K, R)) * 1 / np.sqrt(K) * fk[:, None]).astype(np.float32),
        "temper": (np.random.uniform(0.6, 2.0, (R, 1))).astype(np.float32),
        "og": (np.random.uniform(0.5, 2.0, (R, 1))).astype(np.float32),
        "base": (0.3 * n((R, M))).astype(np.float32),
        "offs": striped(idx),
        "offs2": striped(idx2),
        "offs3": striped(idx3),
        "offs4": striped(idx4),
    }


def reference(dtab_words, dtab_scales, tab_words, tab_scales, w1, temper, og, base, offs, offs2, offs3, offs4):
    idx = unstriped(offs)
    idx2 = unstriped(offs2)
    idx3 = unstriped(offs3)
    idx4 = unstriped(offs4)
    dtabu = unpack_weight(dtab_words, dtab_scales, "e4m3")
    tabu = unpack_weight(tab_words, tab_scales, "e4m3")
    w1q = mxq(f64(w1), 0, "e4m3")
    tabidxg = tabu[:, idx]
    a = w1q.T @ tabidxg
    dtabidxg = dtabu[:, idx]
    ta = w1q.T @ dtabidxg
    e1s = np.exp(a * f64(temper) * (-1.0))
    s = e1s[:, idx2] + e1s[:, idx3] + e1s[:, idx4]
    xe1s = ta * f64(temper) * (-1.0) * e1s
    xs = xe1s[:, idx2] + xe1s[:, idx3] + xe1s[:, idx4]
    xu1 = xs / s / f64(temper) * (-1.0)
    y = xu1 * f64(og) + f64(base)
    return y

@@ -1,0 +1,121 @@
+from contextlib import ExitStack
+
+import concourse.mybir as mybir
+
+K, R, T, J, M = 512, 128, 2048, 512, 256
+FLOPS = 2 * 2 * K * R * J
+
+F32 = mybir.dt.float32
+BF16 = mybir.dt.bfloat16
+I32 = mybir.dt.int32
+U32 = mybir.dt.uint32
+U16 = mybir.dt.uint16
+U8 = mybir.dt.uint8
+FP8X4 = mybir.dt.float8_e4m3fn_x4
+ACT = mybir.ActivationFunctionType
+ALU = mybir.AluOpType
+
+P = 128
+PACK = 4
+HALF = J // 2
+
+
+def tile_attend_tcsoftleast_kernel(tc, dtab_words, dtab_scales, tab_words, tab_scales, w1, temper, og, base, offs, offs2, offs3, offs4, out):
+    nc = tc.nc
+    with ExitStack() as ctx:
+        sb = ctx.enter_context(tc.tile_pool(name="sb", bufs=1))
+        ps = ctx.enter_context(tc.psum_pool(name="ps", bufs=1))
+
+        slots = sb.tile([P, J // 16], U16, name="slots")
+        picks = [sb.tile([P, M // 16], U16, name="picks%d" % i) for i in range(3)]
+        tab_w = sb.tile([P, T], I32, name="tab_w", align_bytes=64)
+        dtab_w = sb.tile([P, T], I32, name="dtab_w", align_bytes=64)
+        tab_s = sb.tile([P, T], U8, name="tab_s", align_bytes=64)
+        dtab_s = sb.tile([P, T], U8, name="dtab_s", align_bytes=64)
+        w_raw = sb.tile([P, PACK, R], F32, name="w_raw")
+        temper_sb = sb.tile([P, 1], F32, name="temper_sb")
+        og_sb = sb.tile([P, 1], F32, name="og_sb")
+        base_sb = sb.tile([P, M], F32, name="base_sb")
+
+        def load_words(tile, words):
+            nc.sync.dma_start(out=tile[:], in_=words[0].rearrange("p n t -> p (n t)").bitcast(I32))
+
+        def load_scales(tile, scales, first):
+            rows = scales[0].bitcast(I32)
+            for i in range(4):
+                nc.scalar.dma_start(out=tile[:].bitcast(I32)[first + i : P : 32, :], in_=rows[i:16:4, :])
+
+        nc.vector.memset(tab_s[:].bitcast(I32), 0)
+        nc.vector.memset(dtab_s[:].bitcast(I32), 0)
+        nc.sync.dma_start(slots[:], offs)
+        load_scales(tab_s, tab_scales, 0)
+        load_words(tab_w, tab_words)
+        nc.sync.dma_start(out=w_raw[:], in_=w1.rearrange("(p j) r -> p j r", j=PACK))
+        nc.gpsimd.dma_start(out=temper_sb[:], in_=temper)
+        nc.sync.dma_start(picks[0][:], offs2)
+        load_scales(dtab_s, dtab_scales, 4)
+        load_words(dtab_w, dtab_words)
+        nc.sync.dma_start(picks[1][:], offs3)
+        nc.sync.dma_start(picks[2][:], offs4)
+        nc.gpsimd.dma_start(out=og_sb[:], in_=og)
+        nc.gpsimd.dma_start(out=base_sb[:], in_=base)
+
+        tab_gs = sb.tile([P, J], U8, name="tab_gs", align_bytes=64)
+        nc.vector.tensor_copy(tab_gs[:], tab_s[:].indirect(slots[:]))
+
+        w_bf = sb.tile([P, R, PACK], BF16, name="w_bf", align_bytes=64)
+        nc.scalar.copy(out=w_bf[:], in_=w_raw[:].rearrange("p j r -> p r j"))
+        neg_temper = sb.tile([P, 1], F32, name="neg_temper")
+        nc.scalar.mul(neg_temper[:], temper_sb[:], -1.0)
+        w_codes = sb.tile([P, R], U32, name="w_codes", align_bytes=64)
+        w_scales = sb.tile([P, R], U8, name="w_scales", align_bytes=64)
+        nc.vector.quantize_mx(out=w_codes[:].bitcast(FP8X4), scales=w_scales[:], in_=w_bf[:].rearrange("p r j -> p (r j)"))
+
+        e1s = sb.tile([P, J], F32, name="e1s")
+        for h in range(2):
+            cols = slice(h * HALF, (h + 1) * HALF)
+            tab_gw = sb.tile([P, HALF], U32, name="tab_gw%d" % h, align_bytes=64)
+            nc.vector.tensor_copy(tab_gw[:], tab_w[:].bitcast(U32).indirect(slots[:, h * HALF // 16 : (h + 1) * HALF // 16]))
+            a_ps = ps.tile([P, HALF], F32, name="a_ps%d" % h)
+            nc.tensor.matmul_mx(out=a_ps[:], lhsT=w_codes[:].bitcast(FP8X4), lhsT_scale=w_scales[:], rhs=tab_gw[:].bitcast(FP8X4), rhs_scale=tab_gs[:, cols], start=True, stop=True)
+            nc.scalar.activation(e1s[:, cols], a_ps[:], ACT.Exp, scale=neg_temper[:])
+
+        dtab_gs = sb.tile([P, J], U8, name="dtab_gs", align_bytes=64)
+        nc.vector.tensor_copy(dtab_gs[:], dtab_s[:].indirect(slots[:]))
+        inv_neg_temper = sb.tile([P, 1], F32, name="inv_neg_temper")
+        nc.vector.reciprocal(inv_neg_temper[:], neg_temper[:])
+        gain = sb.tile([P, 1], F32, name="gain")
+        nc.scalar.activation(gain[:], og_sb[:], ACT.Copy, scale=inv_neg_temper[:])
+
+        def picked(window, i, name, partial):
+            total = sb.tile([P, M], F32, name=name)
+            if partial is None:
+                nc.vector.tensor_copy(total[:], window[:].indirect(picks[i][:]))
+            else:
+                nc.vector.tensor_tensor(total[:], window[:].indirect(picks[i][:]), partial[:], ALU.add)
+            return total
+
+        s = picked(e1s, 0, "s0", None)
+        dtab_gw = sb.tile([P, J], U32, name="dtab_gw", align_bytes=64)
+        nc.vector.tensor_copy(dtab_gw[:], dtab_w[:].bitcast(U32).indirect(slots[:]))
+        ta_ps = ps.tile([P, J], F32, name="ta_ps")
+        nc.tensor.matmul_mx(out=ta_ps[:], lhsT=w_codes[:].bitcast(FP8X4), lhsT_scale=w_scales[:], rhs=dtab_gw[:].bitcast(FP8X4), rhs_scale=dtab_gs[4:P, :], start=True, stop=True)
+        s = picked(e1s, 1, "s1", s)
+        s = picked(e1s, 2, "s2", s)
+
+        root = sb.tile([P, M], F32, name="root")
+        nc.scalar.activation(root[:], s[:], ACT.Abs_reciprocal_sqrt)
+        inv_s = sb.tile([P, M], F32, name="inv_s")
+        nc.scalar.activation(inv_s[:], root[:], ACT.Square)
+
+        xe1s = sb.tile([P, J], F32, name="xe1s")
+        nc.vector.scalar_tensor_tensor(xe1s[:], ta_ps[:], neg_temper[:], e1s[:], ALU.mult, ALU.mult)
+        xs = picked(xe1s, 0, "xs0", None)
+        xs = picked(xe1s, 1, "xs1", xs)
+        xs = picked(xe1s, 2, "xs2", xs)
+
+        scaled = sb.tile([P, M], F32, name="scaled")
+        nc.vector.scalar_tensor_tensor(scaled[:], xs[:], gain[:], inv_s[:], ALU.mult, ALU.mult)
+        y = sb.tile([P, M], F32, name="y")
+        nc.vector.tensor_tensor(y[:], scaled[:], base_sb[:], ALU.add)
+        nc.sync.dma_start(out=out, in_=y[:])

@@ -37,85 +37,101 @@ def tile_attend_tcsoftleast_kernel(tc, dtab_words, dtab_scales, tab_words, tab_s
         og_sb = sb.tile([P, 1], F32, name="og_sb")
         base_sb = sb.tile([P, M], F32, name="base_sb")
 
-        def load_words(tile, words):
-            nc.sync.dma_start(out=tile[:], in_=words[0].rearrange("p n t -> p (n t)").bitcast(I32))
+        def load_words(queue, tile, words):
+            queue.dma_start(out=tile[:], in_=words[0].rearrange("p n t -> p (n t)").bitcast(I32))
 
-        def load_scales(tile, scales, first):
-            rows = scales[0].bitcast(I32)
-            for i in range(4):
-                nc.scalar.dma_start(out=tile[:].bitcast(I32)[first + i : P : 32, :], in_=rows[i:16:4, :])
+        def load_scales(queue, tile, scales, first, i):
+            queue.dma_start(out=tile[:].bitcast(I32)[first + i : P : 32, :], in_=scales[0].bitcast(I32)[i:16:4, :])
 
-        nc.vector.memset(tab_s[:].bitcast(I32), 0)
+        nc.vector.memset(tab_s[:, : T // 2].bitcast(I32), 0)
+        nc.gpsimd.memset(tab_s[:, T // 2 :].bitcast(I32), 0)
         nc.vector.memset(dtab_s[:].bitcast(I32), 0)
         nc.sync.dma_start(slots[:], offs)
-        load_scales(tab_s, tab_scales, 0)
-        load_words(tab_w, tab_words)
-        nc.sync.dma_start(out=w_raw[:], in_=w1.rearrange("(p j) r -> p j r", j=PACK))
-        nc.gpsimd.dma_start(out=temper_sb[:], in_=temper)
-        nc.sync.dma_start(picks[0][:], offs2)
-        load_scales(dtab_s, dtab_scales, 4)
-        load_words(dtab_w, dtab_words)
-        nc.sync.dma_start(picks[1][:], offs3)
-        nc.sync.dma_start(picks[2][:], offs4)
+        nc.scalar.dma_start(out=temper_sb[:], in_=temper)
+        nc.scalar.dma_start(out=w_raw[:], in_=w1.rearrange("(p j) r -> p j r", j=PACK))
+        for i in range(3):
+            load_scales(nc.sync, tab_s, tab_scales, 0, i)
+        load_scales(nc.scalar, tab_s, tab_scales, 0, 3)
+        load_words(nc.scalar, tab_w, tab_words)
+        load_words(nc.scalar, dtab_w, dtab_words)
+        for i in range(4):
+            load_scales(nc.sync, dtab_s, dtab_scales, 4, i)
+        for tile, given in zip(picks, (offs2, offs3, offs4)):
+            nc.sync.dma_start(tile[:], given)
         nc.gpsimd.dma_start(out=og_sb[:], in_=og)
         nc.gpsimd.dma_start(out=base_sb[:], in_=base)
 
-        tab_gs = sb.tile([P, J], U8, name="tab_gs", align_bytes=64)
-        nc.vector.tensor_copy(tab_gs[:], tab_s[:].indirect(slots[:]))
-
         w_bf = sb.tile([P, R, PACK], BF16, name="w_bf", align_bytes=64)
-        nc.scalar.copy(out=w_bf[:], in_=w_raw[:].rearrange("p j r -> p r j"))
+        nc.vector.tensor_copy(out=w_bf[:], in_=w_raw[:].rearrange("p j r -> p r j"))
+        exp_scale = sb.tile([P, 1], F32, name="exp_scale", tag="column")
+        nc.scalar.mul(exp_scale[:], temper_sb[:], -1.0)
         neg_temper = sb.tile([P, 1], F32, name="neg_temper")
         nc.scalar.mul(neg_temper[:], temper_sb[:], -1.0)
+        neg_sign = sb.tile([P, 1], F32, name="neg_sign")
+        nc.scalar.activation(neg_sign[:], temper_sb[:], ACT.Sign, scale=-1.0)
+        gain = sb.tile([P, 1], F32, name="gain")
+        nc.scalar.activation(gain[:], og_sb[:], ACT.Copy, scale=neg_sign[:])
         w_codes = sb.tile([P, R], U32, name="w_codes", align_bytes=64)
         w_scales = sb.tile([P, R], U8, name="w_scales", align_bytes=64)
         nc.vector.quantize_mx(out=w_codes[:].bitcast(FP8X4), scales=w_scales[:], in_=w_bf[:].rearrange("p r j -> p (r j)"))
 
+        tab_gs = sb.tile([P, J], U8, name="tab_gs", align_bytes=64)
+        nc.vector.tensor_copy(tab_gs[:], tab_s[:].indirect(slots[:]))
+
         e1s = sb.tile([P, J], F32, name="e1s")
         for h in range(2):
             cols = slice(h * HALF, (h + 1) * HALF)
-            tab_gw = sb.tile([P, HALF], U32, name="tab_gw%d" % h, align_bytes=64)
+            tab_gw = sb.tile([P, HALF], U32, name="tab_gw%d" % h, tag="gathered%d" % h, align_bytes=64)
             nc.vector.tensor_copy(tab_gw[:], tab_w[:].bitcast(U32).indirect(slots[:, h * HALF // 16 : (h + 1) * HALF // 16]))
             a_ps = ps.tile([P, HALF], F32, name="a_ps%d" % h)
             nc.tensor.matmul_mx(out=a_ps[:], lhsT=w_codes[:].bitcast(FP8X4), lhsT_scale=w_scales[:], rhs=tab_gw[:].bitcast(FP8X4), rhs_scale=tab_gs[:, cols], start=True, stop=True)
-            nc.scalar.activation(e1s[:, cols], a_ps[:], ACT.Exp, scale=neg_temper[:])
+            nc.scalar.activation(e1s[:, cols], a_ps[:], ACT.Exp, scale=exp_scale[:])
 
-        dtab_gs = sb.tile([P, J], U8, name="dtab_gs", align_bytes=64)
+        temper_root = sb.tile([P, 1], F32, name="temper_root", tag="column")
+        nc.scalar.activation(temper_root[:], temper_sb[:], ACT.Abs_reciprocal_sqrt)
+
+        dtab_gs = sb.tile([P, J], U8, name="dtab_gs", tag="gathered0", align_bytes=64)
         nc.vector.tensor_copy(dtab_gs[:], dtab_s[:].indirect(slots[:]))
-        inv_neg_temper = sb.tile([P, 1], F32, name="inv_neg_temper")
-        nc.vector.reciprocal(inv_neg_temper[:], neg_temper[:])
-        gain = sb.tile([P, 1], F32, name="gain")
-        nc.scalar.activation(gain[:], og_sb[:], ACT.Copy, scale=inv_neg_temper[:])
-
-        def picked(window, i, name, partial):
-            total = sb.tile([P, M], F32, name=name)
-            if partial is None:
-                nc.vector.tensor_copy(total[:], window[:].indirect(picks[i][:]))
-            else:
-                nc.vector.tensor_tensor(total[:], window[:].indirect(picks[i][:]), partial[:], ALU.add)
-            return total
-
-        s = picked(e1s, 0, "s0", None)
         dtab_gw = sb.tile([P, J], U32, name="dtab_gw", align_bytes=64)
         nc.vector.tensor_copy(dtab_gw[:], dtab_w[:].bitcast(U32).indirect(slots[:]))
         ta_ps = ps.tile([P, J], F32, name="ta_ps")
         nc.tensor.matmul_mx(out=ta_ps[:], lhsT=w_codes[:].bitcast(FP8X4), lhsT_scale=w_scales[:], rhs=dtab_gw[:].bitcast(FP8X4), rhs_scale=dtab_gs[4:P, :], start=True, stop=True)
-        s = picked(e1s, 1, "s1", s)
-        s = picked(e1s, 2, "s2", s)
 
-        root = sb.tile([P, M], F32, name="root")
-        nc.scalar.activation(root[:], s[:], ACT.Abs_reciprocal_sqrt)
-        inv_s = sb.tile([P, M], F32, name="inv_s")
-        nc.scalar.activation(inv_s[:], root[:], ACT.Square)
+        parts = [slice(0, M // 2), slice(M // 2, M)]
 
+        def picked(window, i, total, partial):
+            for part in parts:
+                looked_up = window[:].indirect(picks[i][:, part.start // 16 : part.stop // 16])
+                if partial is None:
+                    nc.vector.tensor_copy(total[:, part], looked_up)
+                else:
+                    nc.vector.tensor_tensor(total[:, part], looked_up, partial[:, part], ALU.add)
+
+        s1 = sb.tile([P, M], F32, name="s1")
+        picked(e1s, 0, s1, None)
+        s2 = sb.tile([P, M], F32, name="s2", tag="dtab_w", align_bytes=64)
+        picked(e1s, 1, s2, s1)
         xe1s = sb.tile([P, J], F32, name="xe1s")
         nc.vector.scalar_tensor_tensor(xe1s[:], ta_ps[:], neg_temper[:], e1s[:], ALU.mult, ALU.mult)
-        xs = picked(xe1s, 0, "xs0", None)
-        xs = picked(xe1s, 1, "xs1", xs)
-        xs = picked(xe1s, 2, "xs2", xs)
+        s = sb.tile([P, M], F32, name="s")
+        picked(e1s, 2, s, s2)
+
+        s_root = sb.tile([P, M], F32, name="s_root")
+        nc.scalar.activation(s_root[:], s[:], ACT.Abs_reciprocal_sqrt)
+        inv = sb.tile([P, M], F32, name="inv")
+        nc.scalar.activation(inv[:], s_root[:], ACT.Square, scale=temper_root[:])
+
+        xs1 = sb.tile([P, M], F32, name="xs1")
+        picked(xe1s, 0, xs1, None)
+        xs2 = sb.tile([P, M], F32, name="xs2")
+        picked(xe1s, 1, xs2, xs1)
+        xs = sb.tile([P, M], F32, name="xs")
+        picked(xe1s, 2, xs, xs2)
 
         scaled = sb.tile([P, M], F32, name="scaled")
-        nc.vector.scalar_tensor_tensor(scaled[:], xs[:], gain[:], inv_s[:], ALU.mult, ALU.mult)
         y = sb.tile([P, M], F32, name="y")
-        nc.vector.tensor_tensor(y[:], scaled[:], base_sb[:], ALU.add)
-        nc.sync.dma_start(out=out, in_=y[:])
+        for part in parts:
+            nc.vector.scalar_tensor_tensor(scaled[:, part], xs[:, part], gain[:], inv[:, part], ALU.mult, ALU.mult)
+        for part, queue in zip(parts, (nc.sync, nc.scalar)):
+            nc.vector.tensor_tensor(y[:, part], scaled[:, part], base_sb[:, part], ALU.add)
+            queue.dma_start(out=out[:, part], in_=y[:, part])

@@ -43,34 +43,29 @@ def tile_attend_tcsoftleast_kernel(tc, dtab_words, dtab_scales, tab_words, tab_s
         def load_scales(queue, tile, scales, first, i):
             queue.dma_start(out=tile[:].bitcast(I32)[first + i : P : 32, :], in_=scales[0].bitcast(I32)[i:16:4, :])
 
-        nc.vector.memset(tab_s[:, : T // 2].bitcast(I32), 0)
-        nc.gpsimd.memset(tab_s[:, T // 2 :].bitcast(I32), 0)
+        nc.vector.memset(tab_s[:].bitcast(I32), 0)
         nc.vector.memset(dtab_s[:].bitcast(I32), 0)
         nc.sync.dma_start(slots[:], offs)
-        nc.scalar.dma_start(out=temper_sb[:], in_=temper)
         nc.scalar.dma_start(out=w_raw[:], in_=w1.rearrange("(p j) r -> p j r", j=PACK))
-        for i in range(3):
-            load_scales(nc.sync, tab_s, tab_scales, 0, i)
-        load_scales(nc.scalar, tab_s, tab_scales, 0, 3)
-        load_words(nc.scalar, tab_w, tab_words)
-        load_words(nc.scalar, dtab_w, dtab_words)
+        for i, queue in enumerate((nc.sync, nc.sync, nc.scalar, nc.scalar)):
+            load_scales(queue, tab_s, tab_scales, 0, i)
+        nc.sync.dma_start(out=temper_sb[:], in_=temper)
+        load_words(nc.sync, tab_w, tab_words)
         for i in range(4):
             load_scales(nc.sync, dtab_s, dtab_scales, 4, i)
-        for tile, given in zip(picks, (offs2, offs3, offs4)):
-            nc.sync.dma_start(tile[:], given)
-        nc.gpsimd.dma_start(out=og_sb[:], in_=og)
-        nc.gpsimd.dma_start(out=base_sb[:], in_=base)
+        nc.sync.dma_start(picks[0][:], offs2)
+        load_words(nc.sync, dtab_w, dtab_words)
+        nc.sync.dma_start(picks[1][:], offs3)
+        nc.sync.dma_start(picks[2][:], offs4)
+        nc.sync.dma_start(out=base_sb[:], in_=base)
+        nc.sync.dma_start(out=og_sb[:], in_=og)
 
         w_bf = sb.tile([P, R, PACK], BF16, name="w_bf", align_bytes=64)
         nc.vector.tensor_copy(out=w_bf[:], in_=w_raw[:].rearrange("p j r -> p r j"))
-        exp_scale = sb.tile([P, 1], F32, name="exp_scale", tag="column")
-        nc.scalar.mul(exp_scale[:], temper_sb[:], -1.0)
         neg_temper = sb.tile([P, 1], F32, name="neg_temper")
         nc.scalar.mul(neg_temper[:], temper_sb[:], -1.0)
-        neg_sign = sb.tile([P, 1], F32, name="neg_sign")
-        nc.scalar.activation(neg_sign[:], temper_sb[:], ACT.Sign, scale=-1.0)
-        gain = sb.tile([P, 1], F32, name="gain")
-        nc.scalar.activation(gain[:], og_sb[:], ACT.Copy, scale=neg_sign[:])
+        temper_sq = sb.tile([P, 1], F32, name="temper_sq")
+        nc.scalar.activation(temper_sq[:], temper_sb[:], ACT.Square)
         w_codes = sb.tile([P, R], U32, name="w_codes", align_bytes=64)
         w_scales = sb.tile([P, R], U8, name="w_scales", align_bytes=64)
         nc.vector.quantize_mx(out=w_codes[:].bitcast(FP8X4), scales=w_scales[:], in_=w_bf[:].rearrange("p r j -> p (r j)"))
@@ -81,16 +76,16 @@ def tile_attend_tcsoftleast_kernel(tc, dtab_words, dtab_scales, tab_words, tab_s
         e1s = sb.tile([P, J], F32, name="e1s")
         for h in range(2):
             cols = slice(h * HALF, (h + 1) * HALF)
-            tab_gw = sb.tile([P, HALF], U32, name="tab_gw%d" % h, tag="gathered%d" % h, align_bytes=64)
+            tab_gw = sb.tile([P, HALF], U32, name="tab_gw%d" % h, align_bytes=64)
             nc.vector.tensor_copy(tab_gw[:], tab_w[:].bitcast(U32).indirect(slots[:, h * HALF // 16 : (h + 1) * HALF // 16]))
             a_ps = ps.tile([P, HALF], F32, name="a_ps%d" % h)
             nc.tensor.matmul_mx(out=a_ps[:], lhsT=w_codes[:].bitcast(FP8X4), lhsT_scale=w_scales[:], rhs=tab_gw[:].bitcast(FP8X4), rhs_scale=tab_gs[:, cols], start=True, stop=True)
-            nc.scalar.activation(e1s[:, cols], a_ps[:], ACT.Exp, scale=exp_scale[:])
+            nc.scalar.activation(e1s[:, cols], a_ps[:], ACT.Exp, scale=neg_temper[:])
 
-        temper_root = sb.tile([P, 1], F32, name="temper_root", tag="column")
-        nc.scalar.activation(temper_root[:], temper_sb[:], ACT.Abs_reciprocal_sqrt)
+        gain = sb.tile([P, 1], F32, name="gain")
+        nc.scalar.activation(gain[:], og_sb[:], ACT.Copy, scale=neg_temper[:])
 
-        dtab_gs = sb.tile([P, J], U8, name="dtab_gs", tag="gathered0", align_bytes=64)
+        dtab_gs = sb.tile([P, J], U8, name="dtab_gs", align_bytes=64)
         nc.vector.tensor_copy(dtab_gs[:], dtab_s[:].indirect(slots[:]))
         dtab_gw = sb.tile([P, J], U32, name="dtab_gw", align_bytes=64)
         nc.vector.tensor_copy(dtab_gw[:], dtab_w[:].bitcast(U32).indirect(slots[:]))
@@ -107,7 +102,7 @@ def tile_attend_tcsoftleast_kernel(tc, dtab_words, dtab_scales, tab_words, tab_s
                 else:
                     nc.vector.tensor_tensor(total[:, part], looked_up, partial[:, part], ALU.add)
 
-        s1 = sb.tile([P, M], F32, name="s1")
+        s1 = sb.tile([P, M], F32, name="s1", tag="dtab_s", align_bytes=64)
         picked(e1s, 0, s1, None)
         s2 = sb.tile([P, M], F32, name="s2", tag="dtab_w", align_bytes=64)
         picked(e1s, 1, s2, s1)
@@ -117,9 +112,9 @@ def tile_attend_tcsoftleast_kernel(tc, dtab_words, dtab_scales, tab_words, tab_s
         picked(e1s, 2, s, s2)
 
         s_root = sb.tile([P, M], F32, name="s_root")
-        nc.scalar.activation(s_root[:], s[:], ACT.Abs_reciprocal_sqrt)
+        nc.scalar.activation(s_root[:], s[:], ACT.Abs_reciprocal_sqrt, scale=temper_sq[:])
         inv = sb.tile([P, M], F32, name="inv")
-        nc.scalar.activation(inv[:], s_root[:], ACT.Square, scale=temper_root[:])
+        nc.scalar.activation(inv[:], s_root[:], ACT.Square)
 
         xs1 = sb.tile([P, M], F32, name="xs1")
         picked(xe1s, 0, xs1, None)

@@ -53,8 +53,8 @@ def tile_attend_tcsoftleast_kernel(tc, dtab_words, dtab_scales, tab_words, tab_s
         load_words(nc.sync, tab_w, tab_words)
         for i in range(4):
             load_scales(nc.sync, dtab_s, dtab_scales, 4, i)
-        nc.sync.dma_start(picks[0][:], offs2)
         load_words(nc.sync, dtab_w, dtab_words)
+        nc.sync.dma_start(picks[0][:], offs2)
         nc.sync.dma_start(picks[1][:], offs3)
         nc.sync.dma_start(picks[2][:], offs4)
         nc.sync.dma_start(out=base_sb[:], in_=base)
@@ -64,6 +64,8 @@ def tile_attend_tcsoftleast_kernel(tc, dtab_words, dtab_scales, tab_words, tab_s
         nc.vector.tensor_copy(out=w_bf[:], in_=w_raw[:].rearrange("p j r -> p r j"))
         neg_temper = sb.tile([P, 1], F32, name="neg_temper")
         nc.scalar.mul(neg_temper[:], temper_sb[:], -1.0)
+        xe_scale = sb.tile([P, 1], F32, name="xe_scale", tag="s")
+        nc.scalar.mul(xe_scale[:], temper_sb[:], -1.0)
         temper_sq = sb.tile([P, 1], F32, name="temper_sq")
         nc.scalar.activation(temper_sq[:], temper_sb[:], ACT.Square)
         w_codes = sb.tile([P, R], U32, name="w_codes", align_bytes=64)
@@ -75,15 +77,12 @@ def tile_attend_tcsoftleast_kernel(tc, dtab_words, dtab_scales, tab_words, tab_s
 
         e1s = sb.tile([P, J], F32, name="e1s")
         for h in range(2):
-            cols = slice(h * HALF, (h + 1) * HALF)
             tab_gw = sb.tile([P, HALF], U32, name="tab_gw%d" % h, align_bytes=64)
             nc.vector.tensor_copy(tab_gw[:], tab_w[:].bitcast(U32).indirect(slots[:, h * HALF // 16 : (h + 1) * HALF // 16]))
+            cols = slice(h * HALF, (h + 1) * HALF)
             a_ps = ps.tile([P, HALF], F32, name="a_ps%d" % h)
             nc.tensor.matmul_mx(out=a_ps[:], lhsT=w_codes[:].bitcast(FP8X4), lhsT_scale=w_scales[:], rhs=tab_gw[:].bitcast(FP8X4), rhs_scale=tab_gs[:, cols], start=True, stop=True)
             nc.scalar.activation(e1s[:, cols], a_ps[:], ACT.Exp, scale=neg_temper[:])
-
-        gain = sb.tile([P, 1], F32, name="gain")
-        nc.scalar.activation(gain[:], og_sb[:], ACT.Copy, scale=neg_temper[:])
 
         dtab_gs = sb.tile([P, J], U8, name="dtab_gs", align_bytes=64)
         nc.vector.tensor_copy(dtab_gs[:], dtab_s[:].indirect(slots[:]))
@@ -94,39 +93,40 @@ def tile_attend_tcsoftleast_kernel(tc, dtab_words, dtab_scales, tab_words, tab_s
 
         parts = [slice(0, M // 2), slice(M // 2, M)]
 
-        def picked(window, i, total, partial):
-            for part in parts:
-                looked_up = window[:].indirect(picks[i][:, part.start // 16 : part.stop // 16])
-                if partial is None:
-                    nc.vector.tensor_copy(total[:, part], looked_up)
-                else:
-                    nc.vector.tensor_tensor(total[:, part], looked_up, partial[:, part], ALU.add)
+        def listed(window, i, part):
+            return window[:].indirect(picks[i][:, part.start // 16 : part.stop // 16])
 
-        s1 = sb.tile([P, M], F32, name="s1", tag="dtab_s", align_bytes=64)
-        picked(e1s, 0, s1, None)
-        s2 = sb.tile([P, M], F32, name="s2", tag="dtab_w", align_bytes=64)
-        picked(e1s, 1, s2, s1)
+        s1 = sb.tile([P, M], F32, name="s1", tag="dtab_w", align_bytes=64)
+        for part in parts:
+            nc.vector.tensor_copy(s1[:, part], listed(e1s, 0, part))
+        s2 = sb.tile([P, M], F32, name="s2")
+        for part in parts:
+            nc.vector.tensor_tensor(s2[:, part], listed(e1s, 1, part), s1[:, part], ALU.add)
         xe1s = sb.tile([P, J], F32, name="xe1s")
-        nc.vector.scalar_tensor_tensor(xe1s[:], ta_ps[:], neg_temper[:], e1s[:], ALU.mult, ALU.mult)
+        nc.vector.scalar_tensor_tensor(xe1s[:], ta_ps[:], xe_scale[:], e1s[:], ALU.mult, ALU.mult)
         s = sb.tile([P, M], F32, name="s")
-        picked(e1s, 2, s, s2)
+        for part in parts:
+            nc.vector.tensor_tensor(s[:, part], listed(e1s, 2, part), s2[:, part], ALU.add)
 
         s_root = sb.tile([P, M], F32, name="s_root")
-        nc.scalar.activation(s_root[:], s[:], ACT.Abs_reciprocal_sqrt, scale=temper_sq[:])
         inv = sb.tile([P, M], F32, name="inv")
+        nc.scalar.activation(s_root[:], s[:], ACT.Abs_reciprocal_sqrt, scale=temper_sq[:])
         nc.scalar.activation(inv[:], s_root[:], ACT.Square)
 
         xs1 = sb.tile([P, M], F32, name="xs1")
-        picked(xe1s, 0, xs1, None)
+        for part in parts:
+            nc.vector.tensor_copy(xs1[:, part], listed(xe1s, 0, part))
         xs2 = sb.tile([P, M], F32, name="xs2")
-        picked(xe1s, 1, xs2, xs1)
+        for part in parts:
+            nc.vector.tensor_tensor(xs2[:, part], listed(xe1s, 1, part), xs1[:, part], ALU.add)
         xs = sb.tile([P, M], F32, name="xs")
-        picked(xe1s, 2, xs, xs2)
+        for part in parts:
+            nc.vector.tensor_tensor(xs[:, part], listed(xe1s, 2, part), xs2[:, part], ALU.add)
 
         scaled = sb.tile([P, M], F32, name="scaled")
         y = sb.tile([P, M], F32, name="y")
         for part in parts:
-            nc.vector.scalar_tensor_tensor(scaled[:, part], xs[:, part], gain[:], inv[:, part], ALU.mult, ALU.mult)
+            nc.vector.scalar_tensor_tensor(scaled[:, part], xs[:, part], og_sb[:], inv[:, part], ALU.mult, ALU.mult)
         for part, queue in zip(parts, (nc.sync, nc.scalar)):
-            nc.vector.tensor_tensor(y[:, part], scaled[:, part], base_sb[:, part], ALU.add)
+            nc.vector.scalar_tensor_tensor(y[:, part], scaled[:, part], neg_temper[:], base_sb[:, part], ALU.mult, ALU.add)
             queue.dma_start(out=out[:, part], in_=y[:, part])

from contextlib import ExitStack

import concourse.mybir as mybir

K, R, T, J, M = 512, 128, 2048, 512, 256
FLOPS = 2 * 2 * K * R * J

F32 = mybir.dt.float32
BF16 = mybir.dt.bfloat16
I32 = mybir.dt.int32
U32 = mybir.dt.uint32
U16 = mybir.dt.uint16
U8 = mybir.dt.uint8
FP8X4 = mybir.dt.float8_e4m3fn_x4
ACT = mybir.ActivationFunctionType
ALU = mybir.AluOpType

P = 128
PACK = 4
HALF = J // 2


def tile_attend_tcsoftleast_kernel(tc, dtab_words, dtab_scales, tab_words, tab_scales, w1, temper, og, base, offs, offs2, offs3, offs4, out):
    nc = tc.nc
    with ExitStack() as ctx:
        sb = ctx.enter_context(tc.tile_pool(name="sb", bufs=1))
        ps = ctx.enter_context(tc.psum_pool(name="ps", bufs=1))

        slots = sb.tile([P, J // 16], U16, name="slots")
        picks = [sb.tile([P, M // 16], U16, name="picks%d" % i) for i in range(3)]
        tab_w = sb.tile([P, T], I32, name="tab_w", align_bytes=64)
        dtab_w = sb.tile([P, T], I32, name="dtab_w", align_bytes=64)
        tab_s = sb.tile([P, T], U8, name="tab_s", align_bytes=64)
        dtab_s = sb.tile([P, T], U8, name="dtab_s", align_bytes=64)
        w_raw = sb.tile([P, PACK, R], F32, name="w_raw")
        temper_sb = sb.tile([P, 1], F32, name="temper_sb")
        og_sb = sb.tile([P, 1], F32, name="og_sb")
        base_sb = sb.tile([P, M], F32, name="base_sb")

        def load_words(queue, tile, words):
            queue.dma_start(out=tile[:], in_=words[0].rearrange("p n t -> p (n t)").bitcast(I32))

        def load_scales(queue, tile, scales, first, i):
            queue.dma_start(out=tile[:].bitcast(I32)[first + i : P : 32, :], in_=scales[0].bitcast(I32)[i:16:4, :])

        nc.vector.memset(tab_s[:].bitcast(I32), 0)
        nc.vector.memset(dtab_s[:].bitcast(I32), 0)
        nc.sync.dma_start(slots[:], offs)
        nc.scalar.dma_start(out=w_raw[:], in_=w1.rearrange("(p j) r -> p j r", j=PACK))
        for i, queue in enumerate((nc.sync, nc.sync, nc.scalar, nc.scalar)):
            load_scales(queue, tab_s, tab_scales, 0, i)
        nc.sync.dma_start(out=temper_sb[:], in_=temper)
        load_words(nc.sync, tab_w, tab_words)
        for i in range(4):
            load_scales(nc.sync, dtab_s, dtab_scales, 4, i)
        load_words(nc.sync, dtab_w, dtab_words)
        nc.sync.dma_start(picks[0][:], offs2)
        nc.sync.dma_start(picks[1][:], offs3)
        nc.sync.dma_start(picks[2][:], offs4)
        nc.sync.dma_start(out=base_sb[:], in_=base)
        nc.sync.dma_start(out=og_sb[:], in_=og)

        w_bf = sb.tile([P, R, PACK], BF16, name="w_bf", align_bytes=64)
        nc.vector.tensor_copy(out=w_bf[:], in_=w_raw[:].rearrange("p j r -> p r j"))
        neg_temper = sb.tile([P, 1], F32, name="neg_temper")
        nc.scalar.mul(neg_temper[:], temper_sb[:], -1.0)
        xe_scale = sb.tile([P, 1], F32, name="xe_scale", tag="s")
        nc.scalar.mul(xe_scale[:], temper_sb[:], -1.0)
        temper_sq = sb.tile([P, 1], F32, name="temper_sq")
        nc.scalar.activation(temper_sq[:], temper_sb[:], ACT.Square)
        w_codes = sb.tile([P, R], U32, name="w_codes", align_bytes=64)
        w_scales = sb.tile([P, R], U8, name="w_scales", align_bytes=64)
        nc.vector.quantize_mx(out=w_codes[:].bitcast(FP8X4), scales=w_scales[:], in_=w_bf[:].rearrange("p r j -> p (r j)"))

        tab_gs = sb.tile([P, J], U8, name="tab_gs", align_bytes=64)
        nc.vector.tensor_copy(tab_gs[:], tab_s[:].indirect(slots[:]))

        e1s = sb.tile([P, J], F32, name="e1s")
        for h in range(2):
            tab_gw = sb.tile([P, HALF], U32, name="tab_gw%d" % h, align_bytes=64)
            nc.vector.tensor_copy(tab_gw[:], tab_w[:].bitcast(U32).indirect(slots[:, h * HALF // 16 : (h + 1) * HALF // 16]))
            cols = slice(h * HALF, (h + 1) * HALF)
            a_ps = ps.tile([P, HALF], F32, name="a_ps%d" % h)
            nc.tensor.matmul_mx(out=a_ps[:], lhsT=w_codes[:].bitcast(FP8X4), lhsT_scale=w_scales[:], rhs=tab_gw[:].bitcast(FP8X4), rhs_scale=tab_gs[:, cols], start=True, stop=True)
            nc.scalar.activation(e1s[:, cols], a_ps[:], ACT.Exp, scale=neg_temper[:])

        dtab_gs = sb.tile([P, J], U8, name="dtab_gs", align_bytes=64)
        nc.vector.tensor_copy(dtab_gs[:], dtab_s[:].indirect(slots[:]))
        dtab_gw = sb.tile([P, J], U32, name="dtab_gw", align_bytes=64)
        nc.vector.tensor_copy(dtab_gw[:], dtab_w[:].bitcast(U32).indirect(slots[:]))
        ta_ps = ps.tile([P, J], F32, name="ta_ps")
        nc.tensor.matmul_mx(out=ta_ps[:], lhsT=w_codes[:].bitcast(FP8X4), lhsT_scale=w_scales[:], rhs=dtab_gw[:].bitcast(FP8X4), rhs_scale=dtab_gs[4:P, :], start=True, stop=True)

        parts = [slice(0, M // 2), slice(M // 2, M)]

        def listed(window, i, part):
            return window[:].indirect(picks[i][:, part.start // 16 : part.stop // 16])

        s1 = sb.tile([P, M], F32, name="s1", tag="dtab_w", align_bytes=64)
        for part in parts:
            nc.vector.tensor_copy(s1[:, part], listed(e1s, 0, part))
        s2 = sb.tile([P, M], F32, name="s2")
        for part in parts:
            nc.vector.tensor_tensor(s2[:, part], listed(e1s, 1, part), s1[:, part], ALU.add)
        xe1s = sb.tile([P, J], F32, name="xe1s")
        nc.vector.scalar_tensor_tensor(xe1s[:], ta_ps[:], xe_scale[:], e1s[:], ALU.mult, ALU.mult)
        s = sb.tile([P, M], F32, name="s")
        for part in parts:
            nc.vector.tensor_tensor(s[:, part], listed(e1s, 2, part), s2[:, part], ALU.add)

        s_root = sb.tile([P, M], F32, name="s_root")
        inv = sb.tile([P, M], F32, name="inv")
        nc.scalar.activation(s_root[:], s[:], ACT.Abs_reciprocal_sqrt, scale=temper_sq[:])
        nc.scalar.activation(inv[:], s_root[:], ACT.Square)

        xs1 = sb.tile([P, M], F32, name="xs1")
        for part in parts:
            nc.vector.tensor_copy(xs1[:, part], listed(xe1s, 0, part))
        xs2 = sb.tile([P, M], F32, name="xs2")
        for part in parts:
            nc.vector.tensor_tensor(xs2[:, part], listed(xe1s, 1, part), xs1[:, part], ALU.add)
        xs = sb.tile([P, M], F32, name="xs")
        for part in parts:
            nc.vector.tensor_tensor(xs[:, part], listed(xe1s, 2, part), xs2[:, part], ALU.add)

        scaled = sb.tile([P, M], F32, name="scaled")
        y = sb.tile([P, M], F32, name="y")
        for part in parts:
            nc.vector.scalar_tensor_tensor(scaled[:, part], xs[:, part], og_sb[:], inv[:, part], ALU.mult, ALU.mult)
        for part, queue in zip(parts, (nc.sync, nc.scalar)):
            nc.vector.scalar_tensor_tensor(y[:, part], scaled[:, part], neg_temper[:], base_sb[:, part], ALU.mult, ALU.add)
            queue.dma_start(out=out[:, part], in_=y[:, part])
